import numpy as np
import ml_dtypes


def mxq(x, axis, fmt="e4m3"):
    dtype, down = {"e4m3": (ml_dtypes.float8_e4m3fn, 7), "e5m2": (ml_dtypes.float8_e5m2, 14)}[fmt]
    v = np.moveaxis(np.asarray(x, np.float32).astype(ml_dtypes.bfloat16).astype(np.float64), axis, -1)
    blocks = v.reshape(v.shape[:-1] + (-1, 32))
    amax = np.abs(blocks).max(-1, keepdims=True)
    byte = np.maximum(np.where(amax > 0, np.frexp(amax)[1] - 1 + 127, 0) - down, 1)
    scale = np.exp2(byte - 127.0)
    codes = (blocks / scale).astype(np.float32).astype(dtype).astype(np.float64)
    return np.moveaxis((codes * scale).reshape(v.shape), -1, axis)


WIDE = False


def mx_kscale(k):
    if not WIDE:
        return np.ones(k)
    levels = np.array([10, -10, 5, -5, 0])
    if k % 512:
        return np.exp2(np.random.permutation(np.resize(levels, k // 32))).repeat(32)
    a = np.empty((k // 512, 16))
    for p in range(k // 512):
        a[p, :8] = np.random.permutation(np.resize(levels, 8))
        for g in range(8):
            far = levels[np.abs(levels - a[p, g]) >= 10]
            a[p, g + 8] = far[np.random.randint(len(far))]
    return np.exp2(a.ravel()).repeat(32)


def f64(x):
    return np.asarray(x).astype(np.float64)


def striped(idx):
    return np.tile(np.asarray(idx).reshape(-1, 16).T, (8, 1)).astype(np.uint16)


def unstriped(offs):
    return offs[:16].T.reshape(-1).astype(np.int64)


E2M1 = np.array([0.0, 0.5, 1.0, 1.5, 2.0, 3.0, 4.0, 6.0, -0.0, -0.5, -1.0, -1.5, -2.0, -3.0, -4.0, -6.0])


def pack_weight(w, fmt):
    k, n = w.shape
    w = f64(np.asarray(w, np.float32).astype(ml_dtypes.bfloat16)).reshape(k // 32, 32, n)
    amax = np.abs(w).max(1)
    if fmt == "e4m3":
        byte = np.frexp(amax)[1] - 1 + 127 - 7
    else:
        mant, ex = np.frexp(amax / 6.0)
        byte = np.where(mant > 0.5, ex, ex - 1) + 127
    byte = np.clip(np.where(amax > 0, byte, 1), 1, 254)
    scaled = (w * np.exp2(127.0 - byte)[:, None, :]).reshape(k, n).astype(np.float32)
    by_word = np.ascontiguousarray(scaled.reshape(k // 512, 128, 4, n).transpose(0, 1, 3, 2))
    if fmt == "e4m3":
        words = by_word.astype(ml_dtypes.float8_e4m3fn).view(np.uint8)
    else:
        c = by_word.astype(ml_dtypes.float4_e2m1fn).view(np.uint8) & 0xF
        words = (c[..., 0::2] | (c[..., 1::2] << 4)).reshape(k // 512, 128, 2 * n)
    return np.ascontiguousarray(words), np.ascontiguousarray(byte.astype(np.uint8).reshape(k // 512, 16, n))


def unpack_weight(words, scales, fmt):
    g, _, n = scales.shape
    words = np.ascontiguousarray(words).reshape(g, 128, n, -1)
    if fmt == "e4m3":
        vals = words.view(ml_dtypes.float8_e4m3fn).astype(np.float64)
    else:
        nib = np.empty((g, 128, n, 4), np.uint8)
        nib[..., 0::2] = words & 0xF
        nib[..., 1::2] = words >> 4
        vals = E2M1[nib]
    vals = vals * np.repeat(np.exp2(scales.astype(np.float64) - 127.0), 8, axis=1)[..., None]
    return vals.transpose(0, 1, 3, 2).reshape(g * 512, n)


def sigmoid(v):
    return 1.0 / (1.0 + np.exp(-v))


B, N, T, D, NQ = 1, 512, 2048, 512, 512
DV = 512


def sgn(shape):
    return np.random.uniform(0.5, 2.0, shape) * np.where(np.random.standard_normal(shape) < 0, -1.0, 1.0)


def setup_inputs():
    n = np.random.standard_normal
    idx = np.random.permutation(T)[:B * N]
    s = mx_kscale(D)[:, None]
    u = mx_kscale(N)
    ut = np.ones(T)
    ut[idx] = u
    kp = pack_weight(n((D, T)) / s, "e4m3")
    return {
        "qT": (n((B, D, NQ)) * s * (1.00 / np.sqrt(D))).astype(np.float32),
        "k_words": kp[0],
        "k_scales": kp[1],
        "vT": (n((DV, T)) / ut).astype(np.float32),
        "ts": np.tile(np.random.uniform(0.5, 2.0, 2048), (128, 1)).astype(np.float32),
        "kb": np.tile(n(2048), (128, 1)).astype(np.float32),
        "og": (n((B, NQ, DV))).astype(np.float32),
        "us": (sgn((B, N, 1)) * u[:, None]).astype(np.float32),
        "offs": striped(idx),
    }


def reference(qT, k_words, k_scales, vT, ts, kb, og, us, offs):
    idx = unstriped(offs)
    pick = lambda x, which: x[:, which].reshape(x.shape[0], B, -1).transpose(1, 0, 2)
    k = unpack_weight(k_words, k_scales, "e4m3")
    kg = pick(k, idx)
    qq = mxq(f64(qT), 1, "e4m3")
    a = kg.transpose(0, 2, 1) @ qq
    y = sigmoid(a * pick(f64(ts), idx)[:, :1, :].transpose(0, 2, 1) + pick(f64(kb), idx)[:, :1, :].transpose(0, 2, 1)) * f64(us)
    wq = mxq(y, 1, "e4m3")
    o = wq.transpose(0, 2, 1) @ mxq(pick(f64(vT), idx).transpose(0, 2, 1), 1, "e4m3")
    r_ = o * sigmoid(f64(og)) / 16.0
    return r_

@@ -1,0 +1,213 @@
+from contextlib import ExitStack
+
+import concourse.mybir as mybir
+from concourse.masks import make_identity
+
+F32 = mybir.dt.float32
+BF16 = mybir.dt.bfloat16
+I32 = mybir.dt.int32
+U32 = mybir.dt.uint32
+U16 = mybir.dt.uint16
+U8 = mybir.dt.uint8
+FP8X4 = mybir.dt.float8_e4m3fn_x4
+ACT = mybir.ActivationFunctionType
+ALU = mybir.AluOpType
+
+P = 128
+PACK = 4
+T = 2048
+N = 512
+NQ = 512
+DV = 512
+D = 512
+HALF = NQ // 2
+TILES = 4
+ROW = P - 1
+RUN = 4
+
+FLOPS = 2 * N * D * NQ + 2 * N * NQ * DV
+BYTES = 4 * D * NQ + 4 * P * T + 16 * T + 4 * DV * T + 2 * 4 * T + 2 * 4 * NQ * DV + 4 * N + 2 * P * (N // 16)
+
+
+def tile_attend_atb_sig_topk_kernel(tc, qT, k_words, k_scales, vT, ts, kb, og, us, offs, out):
+    nc = tc.nc
+    with ExitStack() as ctx:
+        sb = ctx.enter_context(tc.tile_pool(name="sb", bufs=1))
+        ps = ctx.enter_context(tc.psum_pool(name="ps", bufs=1))
+
+        def tile(shape, dtype, name, after=None):
+            return sb.tile(shape, dtype, name=name, tag=after or name, align_bytes=64)
+
+        offsets = tile([P, N // 16], U16, "offsets")
+        nc.sync.dma_start(offsets[:], offs)
+
+        ks_win = tile([P, T], U8, "ks_win")
+        ts_win = tile([P, T], F32, "ts_win")
+        kb_win = tile([P, T], F32, "kb_win")
+        nc.gpsimd.memset(ks_win[:].bitcast(I32), 0)
+        nc.vector.memset(ts_win[0:ROW, :], 0.0)
+        nc.vector.memset(kb_win[0:ROW, :], 0.0)
+        nc.sync.dma_start(ts_win[ROW:P, :], ts[0:1, :])
+        nc.sync.dma_start(kb_win[ROW:P, :], kb[0:1, :])
+        zero = tile([P, 1], F32, "zero")
+        nc.gpsimd.memset(zero[:], 0.0)
+        warm = tile([P, 1], F32, "warm")
+        nc.scalar.activation(warm[:], zero[:], ACT.Sigmoid)
+        ident = tile([P, P], F32, "ident")
+        make_identity(nc, ident[:])
+
+        q_raw = tile([P, PACK, NQ], F32, "q_raw")
+        nc.sync.dma_start(q_raw[:], qT[0].rearrange("(p j) q -> p j q", j=PACK))
+        for quad in range(4):
+            nc.sync.dma_start(
+                ks_win[32 * quad : 32 * quad + 4, :].bitcast(I32),
+                k_scales[0, 4 * quad : 4 * quad + 4, :].bitcast(I32),
+            )
+        kw_win = tile([P, T], I32, "kw_win")
+        nc.sync.dma_start(kw_win[:], k_words[0].rearrange("p t r -> p (t r)").bitcast(I32))
+        us_col = tile([P, PACK], F32, "us_col")
+        nc.sync.dma_start(us_col[:], us[0].rearrange("(p t) o -> p (t o)", t=PACK))
+        v_win = []
+        for j in range(TILES):
+            v_win.append(tile([P, T], F32, "v_win%d" % j))
+            nc.sync.dma_start(v_win[j][:], vT[P * j : P * (j + 1), :])
+        og_raw = []
+        for m in range(TILES):
+            og_raw.append(tile([P, DV], F32, "og_raw%d" % m))
+            nc.sync.dma_start(og_raw[m][:], og[0, P * m : P * (m + 1), :])
+
+        q_bf = tile([P, NQ, PACK], BF16, "q_bf")
+        for h in range(2):
+            cols = slice(HALF * h, HALF * (h + 1))
+            nc.scalar.copy(
+                q_bf[:, cols, :].rearrange("p (c i) j -> p c j i", i=RUN),
+                q_raw[:, :, cols].rearrange("p j (c i) -> p c j i", i=RUN),
+            )
+        token_cols = tile([P, 2, PACK], F32, "token_cols", after="q_raw")
+
+        def token_column(win, name, col):
+            picked = tile([P, N], F32, name + "_picked")
+            nc.vector.tensor_copy(picked[:], win[:].indirect(offsets[:]))
+            turned = ps.tile([P, PACK, P], F32, name=name + "_turned", tag=name + "_bank")
+            for t in range(PACK):
+                nc.tensor.transpose(turned[:, t, :], picked[:, t:N:PACK], ident[:])
+            nc.scalar.copy(col, turned[:, :, ROW])
+
+        ts_col = token_cols[:, 0, :]
+        kb_col = token_cols[:, 1, :]
+        token_column(ts_win, "ts", ts_col)
+        token_column(kb_win, "kb", kb_col)
+
+        ks_picked = tile([P, N], U8, "ks_picked")
+        nc.vector.tensor_copy(ks_picked[:], ks_win[:].indirect(offsets[:]))
+        k_scale = tile([P, PACK, P], U8, "k_scale")
+        nc.vector.tensor_copy(
+            k_scale[:].rearrange("p t s -> p s t"), ks_picked[:].rearrange("p (s t) -> p s t", t=PACK)
+        )
+
+        q_code = tile([P, NQ], U32, "q_code")
+        q_scale = tile([P, NQ], U8, "q_scale")
+        nc.vector.quantize_mx(q_code[:].bitcast(FP8X4), q_scale[:], q_bf[:].rearrange("p q j -> p (q j)"))
+
+        k_code = tile([P, PACK, P], U32, "k_code")
+        nc.vector.tensor_copy(k_code[:].rearrange("p t s -> p s t"), kw_win[:].bitcast(U32).indirect(offsets[:]))
+
+        score = []
+        for t in range(PACK):
+            score.append(ps.tile([P, NQ], F32, name="score%d" % t, tag="bank%d" % t))
+            nc.tensor.matmul_mx(
+                score[t][:], k_code[:, t, :].bitcast(FP8X4), k_scale[:, t, :],
+                q_code[:].bitcast(FP8X4), q_scale[:], start=True, stop=True,
+            )
+
+        def weights(h):
+            cols = slice(HALF * h, HALF * (h + 1))
+            sig = tile([P, PACK, HALF], F32, "sig%d" % h)
+            y_flat = tile([P, PACK, HALF], BF16, "y_flat%d" % h)
+            for t in range(PACK):
+                nc.scalar.activation(
+                    sig[:, t, :], score[t][:, cols], ACT.Sigmoid,
+                    bias=kb_col[:, t : t + 1], scale=ts_col[:, t : t + 1],
+                )
+            for t in range(PACK):
+                nc.scalar.activation(y_flat[:, t, :], sig[:, t, :], ACT.Copy, scale=us_col[:, t : t + 1])
+            return y_flat
+
+        def interleave_weights(h, y_flat):
+            y_bf = tile([P, HALF, PACK], BF16, "y_bf%d" % h, after="v_win%d" % (h + 1))
+            nc.vector.tensor_copy(
+                y_bf[:].rearrange("p (c i) t -> p c t i", i=RUN),
+                y_flat[:].rearrange("p t (c i) -> p c t i", i=RUN),
+            )
+            return y_bf
+
+        def quantise(src, name, after=None):
+            width = src.shape[1] // PACK
+            code = tile([P, width], U32, name + "_code", after=after)
+            scale = tile([P, width], U8, name + "_scale")
+            nc.vector.quantize_mx(code[:].bitcast(FP8X4), scale[:], src)
+            return code, scale
+
+        def pick_values(j):
+            picked = tile([P, N], BF16, "v_picked%d" % j)
+            nc.vector.tensor_copy(picked[:], v_win[j][:].indirect(offsets[:]))
+            pairs = picked[:].bitcast(F32)
+            turned = ps.tile([P, 2, P], F32, name="v_turned%d" % j, tag="v_bank%d" % (j % 2))
+            for u in range(2):
+                nc.tensor.transpose(turned[:, u, :], pairs[:, u : N // 2 : 2], ident[:])
+            return turned
+
+        def lay_values(turned, dst):
+            nc.scalar.copy(
+                dst.bitcast(F32).rearrange("p (e u) -> p e u", u=2), turned[:].rearrange("p u e -> p e u")
+            )
+
+        turned0 = pick_values(0)
+        y0 = weights(0)
+        turned1 = pick_values(1)
+        v_bf01 = tile([P, 2 * N], BF16, "v_bf01", after="sig0")
+        lay_values(turned0, v_bf01[:, 0:N])
+        lay_values(turned1, v_bf01[:, N : 2 * N])
+        y_bf0 = interleave_weights(0, y0)
+        y1 = weights(1)
+        vq01 = quantise(v_bf01[:], "v01")
+        yq = [quantise(y_bf0[:].rearrange("p q t -> p (q t)"), "y0")]
+        turned2 = pick_values(2)
+        v_bf2 = tile([P, N], BF16, "v_bf2", after="sig1")
+        lay_values(turned2, v_bf2[:])
+        y_bf1 = interleave_weights(1, y1)
+        vq2 = quantise(v_bf2[:], "v2")
+        turned3 = pick_values(3)
+        yq.append(quantise(y_bf1[:].rearrange("p q t -> p (q t)"), "y1", after="v_win3"))
+
+        def product(dst, m, vq):
+            y_code, y_scale = yq[m // 2]
+            cols = slice(P * (m % 2), P * (m % 2 + 1))
+            nc.tensor.matmul_mx(
+                dst, y_code[:, cols].bitcast(FP8X4), y_scale[:, cols],
+                vq[0][:].bitcast(FP8X4), vq[1][:], start=True, stop=True,
+            )
+
+        gate = tile([P, TILES, DV], F32, "gate")
+        early = P * (TILES - 1)
+        for m in range(TILES):
+            acc = ps.tile([P, early], F32, name="acc%d" % m, tag="bank%d" % m)
+            product(acc[:, 0 : 2 * P], m, vq01)
+            product(acc[:, 2 * P : early], m, vq2)
+            nc.scalar.activation(gate[:, m, :], og_raw[m][:], ACT.Sigmoid)
+            res = tile([P, early], F32, "res%d" % m)
+            nc.vector.scalar_tensor_tensor(res[:], acc[:], 1.0 / 16.0, gate[:, m, 0:early], ALU.mult, ALU.mult)
+            nc.sync.dma_start(out[0, P * m : P * (m + 1), 0:early], res[:])
+            if m == 2:
+                v_bf3 = tile([P, N], BF16, "v_bf3", after="og_raw2")
+                lay_values(turned3, v_bf3[:])
+                vq3 = quantise(v_bf3[:], "v3")
+
+        acc_last = ps.tile([P, TILES, P], F32, name="acc_last", tag="ts_bank")
+        for m in range(TILES):
+            product(acc_last[:, m, :], m, vq3)
+        res_last = tile([P, TILES, P], F32, "res_last")
+        nc.vector.scalar_tensor_tensor(
+            res_last[:], acc_last[:], 1.0 / 16.0, gate[:, :, early:DV], ALU.mult, ALU.mult
+        )
+        nc.sync.dma_start(out[0].rearrange("(m p) e -> p m e", p=P)[:, :, early:DV], res_last[:])

@@ -49,12 +49,13 @@ def tile_attend_atb_sig_topk_kernel(tc, qT, k_words, k_scales, vT, ts, kb, og, u
         nc.vector.memset(kb_win[0:ROW, :], 0.0)
         nc.sync.dma_start(ts_win[ROW:P, :], ts[0:1, :])
         nc.sync.dma_start(kb_win[ROW:P, :], kb[0:1, :])
-        zero = tile([P, 1], F32, "zero")
-        nc.gpsimd.memset(zero[:], 0.0)
-        warm = tile([P, 1], F32, "warm")
-        nc.scalar.activation(warm[:], zero[:], ACT.Sigmoid)
         ident = tile([P, P], F32, "ident")
         make_identity(nc, ident[:])
+
+        gate = tile([P, TILES, DV], F32, "gate")
+        og_first = tile([P, P], F32, "og_first")
+        nc.sync.dma_start(og_first[:], og[0, 0:P, 0:P])
+        nc.scalar.activation(gate[:, 0, 0:P], og_first[:], ACT.Sigmoid)
 
         q_raw = tile([P, PACK, NQ], F32, "q_raw")
         nc.sync.dma_start(q_raw[:], qT[0].rearrange("(p j) q -> p j q", j=PACK))
@@ -73,15 +74,16 @@ def tile_attend_atb_sig_topk_kernel(tc, qT, k_words, k_scales, vT, ts, kb, og, u
             nc.sync.dma_start(v_win[j][:], vT[P * j : P * (j + 1), :])
         og_raw = []
         for m in range(TILES):
-            og_raw.append(tile([P, DV], F32, "og_raw%d" % m))
-            nc.sync.dma_start(og_raw[m][:], og[0, P * m : P * (m + 1), :])
+            first = P if m == 0 else 0
+            og_raw.append(tile([P, DV - first], F32, "og_raw%d" % m))
+            nc.sync.dma_start(og_raw[m][:], og[0, P * m : P * (m + 1), first:DV])
 
-        q_bf = tile([P, NQ, PACK], BF16, "q_bf")
+        q_bf = []
         for h in range(2):
-            cols = slice(HALF * h, HALF * (h + 1))
+            q_bf.append(tile([P, HALF, PACK], BF16, "q_bf%d" % h))
             nc.scalar.copy(
-                q_bf[:, cols, :].rearrange("p (c i) j -> p c j i", i=RUN),
-                q_raw[:, :, cols].rearrange("p j (c i) -> p c j i", i=RUN),
+                q_bf[h][:].rearrange("p (c i) j -> p c j i", i=RUN),
+                q_raw[:, :, HALF * h : HALF * (h + 1)].rearrange("p j (c i) -> p c j i", i=RUN),
             )
         token_cols = tile([P, 2, PACK], F32, "token_cols", after="q_raw")
 
@@ -105,54 +107,63 @@ def tile_attend_atb_sig_topk_kernel(tc, qT, k_words, k_scales, vT, ts, kb, og, u
             k_scale[:].rearrange("p t s -> p s t"), ks_picked[:].rearrange("p (s t) -> p s t", t=PACK)
         )
 
-        q_code = tile([P, NQ], U32, "q_code")
-        q_scale = tile([P, NQ], U8, "q_scale")
-        nc.vector.quantize_mx(q_code[:].bitcast(FP8X4), q_scale[:], q_bf[:].rearrange("p q j -> p (q j)"))
-
-        k_code = tile([P, PACK, P], U32, "k_code")
-        nc.vector.tensor_copy(k_code[:].rearrange("p t s -> p s t"), kw_win[:].bitcast(U32).indirect(offsets[:]))
-
-        score = []
-        for t in range(PACK):
-            score.append(ps.tile([P, NQ], F32, name="score%d" % t, tag="bank%d" % t))
-            nc.tensor.matmul_mx(
-                score[t][:], k_code[:, t, :].bitcast(FP8X4), k_scale[:, t, :],
-                q_code[:].bitcast(FP8X4), q_scale[:], start=True, stop=True,
-            )
-
-        def weights(h):
-            cols = slice(HALF * h, HALF * (h + 1))
-            sig = tile([P, PACK, HALF], F32, "sig%d" % h)
-            y_flat = tile([P, PACK, HALF], BF16, "y_flat%d" % h)
-            for t in range(PACK):
-                nc.scalar.activation(
-                    sig[:, t, :], score[t][:, cols], ACT.Sigmoid,
-                    bias=kb_col[:, t : t + 1], scale=ts_col[:, t : t + 1],
-                )
-            for t in range(PACK):
-                nc.scalar.activation(y_flat[:, t, :], sig[:, t, :], ACT.Copy, scale=us_col[:, t : t + 1])
-            return y_flat
-
-        def interleave_weights(h, y_flat):
-            y_bf = tile([P, HALF, PACK], BF16, "y_bf%d" % h, after="v_win%d" % (h + 1))
-            nc.vector.tensor_copy(
-                y_bf[:].rearrange("p (c i) t -> p c t i", i=RUN),
-                y_flat[:].rearrange("p t (c i) -> p c t i", i=RUN),
-            )
-            return y_bf
-
-        def quantise(src, name, after=None):
-            width = src.shape[1] // PACK
-            code = tile([P, width], U32, name + "_code", after=after)
-            scale = tile([P, width], U8, name + "_scale")
-            nc.vector.quantize_mx(code[:].bitcast(FP8X4), scale[:], src)
+        def quantise(src, code, name):
+            scale = tile([P, src.shape[1] // PACK], U8, name + "_scale")
+            nc.vector.quantize_mx(code.bitcast(FP8X4), scale[:], src)
             return code, scale
 
+        def flat(woven):
+            return woven[:].rearrange("p q t -> p (q t)")
+
+        q_code0 = tile([P, HALF], U32, "q_code0", after="ks_win")
+        qq = [quantise(flat(q_bf[0]), q_code0[:], "q0")]
+        k_code = tile([P, PACK, P], U32, "k_code", after="ks_picked")
+        nc.vector.tensor_copy(k_code[:].rearrange("p t s -> p s t"), kw_win[:].bitcast(U32).indirect(offsets[:]))
+        q_code1 = tile([P, HALF], U32, "q_code1", after="kw_win")
+        qq.append(quantise(flat(q_bf[1]), q_code1[:], "q1"))
+
+        def sigmoids(h):
+            sig = tile([P, PACK, HALF], F32, "sig%d" % h)
+            banks = []
+            for pair in range(2):
+                banks.append(ps.tile([P, 2, HALF], F32, name="score%d%d" % (h, pair), tag="bank%d" % (2 * h + pair)))
+            for t in range(PACK):
+                nc.tensor.matmul_mx(
+                    banks[t // 2][:, t % 2, :], k_code[:, t, :].bitcast(FP8X4), k_scale[:, t, :],
+                    qq[h][0].bitcast(FP8X4), qq[h][1][:], start=True, stop=True,
+                )
+            for t in range(PACK):
+                nc.scalar.activation(
+                    sig[:, t, :], banks[t // 2][:, t % 2, :], ACT.Sigmoid,
+                    bias=kb_col[:, t : t + 1], scale=ts_col[:, t : t + 1],
+                )
+            return sig
+
+        def by_run(rows):
+            return rows[:].rearrange("p t (c i) -> p c t i", i=RUN)
+
+        def by_word(woven):
+            return woven[:].rearrange("p (c i) t -> p c t i", i=RUN)
+
+        def weave_on_vector(sig):
+            y_bf = tile([P, HALF, PACK], BF16, "y_bf0", after="v_win1")
+            factor = us_col[:].unsqueeze(1).unsqueeze(3).to_broadcast([P, HALF // RUN, PACK, RUN])
+            nc.vector.tensor_tensor(by_word(y_bf), by_run(sig), factor, ALU.mult)
+            return y_bf
+
+        def weave_on_scalar(sig):
+            y_flat = tile([P, PACK, HALF], BF16, "y_flat")
+            for t in range(PACK):
+                nc.scalar.activation(y_flat[:, t, :], sig[:, t, :], ACT.Copy, scale=us_col[:, t : t + 1])
+            y_bf = tile([P, HALF, PACK], BF16, "y_bf1")
+            nc.scalar.copy(by_word(y_bf), by_run(y_flat))
+            return y_bf
+
         def pick_values(j):
-            picked = tile([P, N], BF16, "v_picked%d" % j)
+            picked = tile([P, N], BF16, "v_picked%d" % j, after="q_bf1" if j == 0 else None)
             nc.vector.tensor_copy(picked[:], v_win[j][:].indirect(offsets[:]))
             pairs = picked[:].bitcast(F32)
-            turned = ps.tile([P, 2, P], F32, name="v_turned%d" % j, tag="v_bank%d" % (j % 2))
+            turned = ps.tile([P, 2, P], F32, name="v_turned%d" % j, tag=("bank1", "bank2", "v_bank0", "v_bank1")[j])
             for u in range(2):
                 nc.tensor.transpose(turned[:, u, :], pairs[:, u : N // 2 : 2], ident[:])
             return turned
@@ -162,52 +173,68 @@ def tile_attend_atb_sig_topk_kernel(tc, qT, k_words, k_scales, vT, ts, kb, og, u
                 dst.bitcast(F32).rearrange("p (e u) -> p e u", u=2), turned[:].rearrange("p u e -> p e u")
             )
 
+        sig0 = sigmoids(0)
+        sig1 = sigmoids(1)
         turned0 = pick_values(0)
-        y0 = weights(0)
         turned1 = pick_values(1)
-        v_bf01 = tile([P, 2 * N], BF16, "v_bf01", after="sig0")
+        v_bf01 = tile([P, 2 * N], BF16, "v_bf01")
         lay_values(turned0, v_bf01[:, 0:N])
         lay_values(turned1, v_bf01[:, N : 2 * N])
-        y_bf0 = interleave_weights(0, y0)
-        y1 = weights(1)
-        vq01 = quantise(v_bf01[:], "v01")
-        yq = [quantise(y_bf0[:].rearrange("p q t -> p (q t)"), "y0")]
+        y_bf0 = weave_on_vector(sig0)
+        y_bf1 = weave_on_scalar(sig1)
         turned2 = pick_values(2)
-        v_bf2 = tile([P, N], BF16, "v_bf2", after="sig1")
-        lay_values(turned2, v_bf2[:])
-        y_bf1 = interleave_weights(1, y1)
-        vq2 = quantise(v_bf2[:], "v2")
+        codes_a = tile([P, HALF + 2 * P], U32, "codes_a", after="v_win2")
+        yq = [quantise(flat(y_bf0), codes_a[:, 0:HALF], "y0")]
+        vq01 = quantise(v_bf01[:], codes_a[:, HALF : HALF + 2 * P], "v01")
         turned3 = pick_values(3)
-        yq.append(quantise(y_bf1[:].rearrange("p q t -> p (q t)"), "y1", after="v_win3"))
+        y_code1 = tile([P, HALF], U32, "y_code1", after="v_win3")
+        yq.append(quantise(flat(y_bf1), y_code1[:], "y1"))
 
         def product(dst, m, vq):
             y_code, y_scale = yq[m // 2]
             cols = slice(P * (m % 2), P * (m % 2 + 1))
             nc.tensor.matmul_mx(
                 dst, y_code[:, cols].bitcast(FP8X4), y_scale[:, cols],
-                vq[0][:].bitcast(FP8X4), vq[1][:], start=True, stop=True,
+                vq[0].bitcast(FP8X4), vq[1][:], start=True, stop=True,
             )
 
-        gate = tile([P, TILES, DV], F32, "gate")
-        early = P * (TILES - 1)
-        for m in range(TILES):
-            acc = ps.tile([P, early], F32, name="acc%d" % m, tag="bank%d" % m)
-            product(acc[:, 0 : 2 * P], m, vq01)
-            product(acc[:, 2 * P : early], m, vq2)
-            nc.scalar.activation(gate[:, m, :], og_raw[m][:], ACT.Sigmoid)
-            res = tile([P, early], F32, "res%d" % m)
-            nc.vector.scalar_tensor_tensor(res[:], acc[:], 1.0 / 16.0, gate[:, m, 0:early], ALU.mult, ALU.mult)
-            nc.sync.dma_start(out[0, P * m : P * (m + 1), 0:early], res[:])
-            if m == 2:
-                v_bf3 = tile([P, N], BF16, "v_bf3", after="og_raw2")
-                lay_values(turned3, v_bf3[:])
-                vq3 = quantise(v_bf3[:], "v3")
+        out_rows = out[0].rearrange("(m p) e -> p m e", p=P)
+        low, high = slice(0, 2 * P), slice(2 * P, DV)
 
-        acc_last = ps.tile([P, TILES, P], F32, name="acc_last", tag="ts_bank")
-        for m in range(TILES):
-            product(acc_last[:, m, :], m, vq3)
-        res_last = tile([P, TILES, P], F32, "res_last")
-        nc.vector.scalar_tensor_tensor(
-            res_last[:], acc_last[:], 1.0 / 16.0, gate[:, :, early:DV], ALU.mult, ALU.mult
-        )
-        nc.sync.dma_start(out[0].rearrange("(m p) e -> p m e", p=P)[:, :, early:DV], res_last[:])
+        def make_gate(m):
+            nc.scalar.activation(gate[:, m, DV - og_raw[m].shape[1] : DV], og_raw[m][:], ACT.Sigmoid)
+
+        def gated(name, acc, rows, cols):
+            res = tile(list(acc.shape), F32, name)
+            nc.vector.scalar_tensor_tensor(res[:], acc, 1.0 / 16.0, gate[:, rows, cols], ALU.mult, ALU.mult)
+            nc.sync.dma_start(out_rows[:, rows, cols], res[:])
+
+        def pair_block(name, bank, vq):
+            acc = ps.tile([P, 2, 2 * P], F32, name=name, tag=bank)
+            for m in range(2):
+                product(acc[:, m, :], m, vq)
+            return acc
+
+        make_gate(0)
+        make_gate(1)
+        acc01_low = pair_block("acc01_low", "bank0", vq01)
+        acc2_low = ps.tile([P, 2 * P], F32, name="acc2_low", tag="bank1")
+        product(acc2_low[:], 2, vq01)
+        acc3 = ps.tile([P, DV], F32, name="acc3", tag="bank3")
+        product(acc3[:, low], 3, vq01)
+        gated("res01_low", acc01_low[:], slice(0, 2), low)
+        v_bf23 = tile([P, 2 * N], BF16, "v_bf23", after="og_raw1")
+        lay_values(turned2, v_bf23[:, 0:N])
+        lay_values(turned3, v_bf23[:, N : 2 * N])
+        v_code23 = tile([P, 2 * P], U32, "v_code23")
+        vq23 = quantise(v_bf23[:], v_code23[:], "v23")
+        make_gate(2)
+        make_gate(3)
+        acc01_high = pair_block("acc01_high", "bank2", vq23)
+        acc2_high = ps.tile([P, 2 * P], F32, name="acc2_high", tag="ts_bank")
+        product(acc2_high[:], 2, vq23)
+        product(acc3[:, high], 3, vq23)
+        gated("res2_low", acc2_low[:], 2, low)
+        gated("res01_high", acc01_high[:], slice(0, 2), high)
+        gated("res2_high", acc2_high[:], 2, high)
+        gated("res3", acc3[:], 3, slice(0, DV))

from contextlib import ExitStack

import concourse.mybir as mybir
from concourse.masks import make_identity

F32 = mybir.dt.float32
BF16 = mybir.dt.bfloat16
I32 = mybir.dt.int32
U32 = mybir.dt.uint32
U16 = mybir.dt.uint16
U8 = mybir.dt.uint8
FP8X4 = mybir.dt.float8_e4m3fn_x4
ACT = mybir.ActivationFunctionType
ALU = mybir.AluOpType

P = 128
PACK = 4
T = 2048
N = 512
NQ = 512
DV = 512
D = 512
HALF = NQ // 2
TILES = 4
ROW = P - 1
RUN = 4

FLOPS = 2 * N * D * NQ + 2 * N * NQ * DV
BYTES = 4 * D * NQ + 4 * P * T + 16 * T + 4 * DV * T + 2 * 4 * T + 2 * 4 * NQ * DV + 4 * N + 2 * P * (N // 16)


def tile_attend_atb_sig_topk_kernel(tc, qT, k_words, k_scales, vT, ts, kb, og, us, offs, out):
    nc = tc.nc
    with ExitStack() as ctx:
        sb = ctx.enter_context(tc.tile_pool(name="sb", bufs=1))
        ps = ctx.enter_context(tc.psum_pool(name="ps", bufs=1))

        def tile(shape, dtype, name, after=None):
            return sb.tile(shape, dtype, name=name, tag=after or name, align_bytes=64)

        offsets = tile([P, N // 16], U16, "offsets")
        nc.sync.dma_start(offsets[:], offs)

        ks_win = tile([P, T], U8, "ks_win")
        ts_win = tile([P, T], F32, "ts_win")
        kb_win = tile([P, T], F32, "kb_win")
        nc.gpsimd.memset(ks_win[:].bitcast(I32), 0)
        nc.vector.memset(ts_win[0:ROW, :], 0.0)
        nc.vector.memset(kb_win[0:ROW, :], 0.0)
        nc.sync.dma_start(ts_win[ROW:P, :], ts[0:1, :])
        nc.sync.dma_start(kb_win[ROW:P, :], kb[0:1, :])
        ident = tile([P, P], F32, "ident")
        make_identity(nc, ident[:])

        gate = tile([P, TILES, DV], F32, "gate")
        og_first = tile([P, P], F32, "og_first")
        nc.sync.dma_start(og_first[:], og[0, 0:P, 0:P])
        nc.scalar.activation(gate[:, 0, 0:P], og_first[:], ACT.Sigmoid)

        q_raw = tile([P, PACK, NQ], F32, "q_raw")
        nc.sync.dma_start(q_raw[:], qT[0].rearrange("(p j) q -> p j q", j=PACK))
        for quad in range(4):
            nc.sync.dma_start(
                ks_win[32 * quad : 32 * quad + 4, :].bitcast(I32),
                k_scales[0, 4 * quad : 4 * quad + 4, :].bitcast(I32),
            )
        kw_win = tile([P, T], I32, "kw_win")
        nc.sync.dma_start(kw_win[:], k_words[0].rearrange("p t r -> p (t r)").bitcast(I32))
        us_col = tile([P, PACK], F32, "us_col")
        nc.sync.dma_start(us_col[:], us[0].rearrange("(p t) o -> p (t o)", t=PACK))
        v_win = []
        for j in range(TILES):
            v_win.append(tile([P, T], F32, "v_win%d" % j))
            nc.sync.dma_start(v_win[j][:], vT[P * j : P * (j + 1), :])
        og_raw = []
        for m in range(TILES):
            first = P if m == 0 else 0
            og_raw.append(tile([P, DV - first], F32, "og_raw%d" % m))
            nc.sync.dma_start(og_raw[m][:], og[0, P * m : P * (m + 1), first:DV])

        q_bf = []
        for h in range(2):
            q_bf.append(tile([P, HALF, PACK], BF16, "q_bf%d" % h))
            nc.scalar.copy(
                q_bf[h][:].rearrange("p (c i) j -> p c j i", i=RUN),
                q_raw[:, :, HALF * h : HALF * (h + 1)].rearrange("p j (c i) -> p c j i", i=RUN),
            )
        token_cols = tile([P, 2, PACK], F32, "token_cols", after="q_raw")

        def token_column(win, name, col):
            picked = tile([P, N], F32, name + "_picked")
            nc.vector.tensor_copy(picked[:], win[:].indirect(offsets[:]))
            turned = ps.tile([P, PACK, P], F32, name=name + "_turned", tag=name + "_bank")
            for t in range(PACK):
                nc.tensor.transpose(turned[:, t, :], picked[:, t:N:PACK], ident[:])
            nc.scalar.copy(col, turned[:, :, ROW])

        ts_col = token_cols[:, 0, :]
        kb_col = token_cols[:, 1, :]
        token_column(ts_win, "ts", ts_col)
        token_column(kb_win, "kb", kb_col)

        ks_picked = tile([P, N], U8, "ks_picked")
        nc.vector.tensor_copy(ks_picked[:], ks_win[:].indirect(offsets[:]))
        k_scale = tile([P, PACK, P], U8, "k_scale")
        nc.vector.tensor_copy(
            k_scale[:].rearrange("p t s -> p s t"), ks_picked[:].rearrange("p (s t) -> p s t", t=PACK)
        )

        def quantise(src, code, name):
            scale = tile([P, src.shape[1] // PACK], U8, name + "_scale")
            nc.vector.quantize_mx(code.bitcast(FP8X4), scale[:], src)
            return code, scale

        def flat(woven):
            return woven[:].rearrange("p q t -> p (q t)")

        q_code0 = tile([P, HALF], U32, "q_code0", after="ks_win")
        qq = [quantise(flat(q_bf[0]), q_code0[:], "q0")]
        k_code = tile([P, PACK, P], U32, "k_code", after="ks_picked")
        nc.vector.tensor_copy(k_code[:].rearrange("p t s -> p s t"), kw_win[:].bitcast(U32).indirect(offsets[:]))
        q_code1 = tile([P, HALF], U32, "q_code1", after="kw_win")
        qq.append(quantise(flat(q_bf[1]), q_code1[:], "q1"))

        def sigmoids(h):
            sig = tile([P, PACK, HALF], F32, "sig%d" % h)
            banks = []
            for pair in range(2):
                banks.append(ps.tile([P, 2, HALF], F32, name="score%d%d" % (h, pair), tag="bank%d" % (2 * h + pair)))
            for t in range(PACK):
                nc.tensor.matmul_mx(
                    banks[t // 2][:, t % 2, :], k_code[:, t, :].bitcast(FP8X4), k_scale[:, t, :],
                    qq[h][0].bitcast(FP8X4), qq[h][1][:], start=True, stop=True,
                )
            for t in range(PACK):
                nc.scalar.activation(
                    sig[:, t, :], banks[t // 2][:, t % 2, :], ACT.Sigmoid,
                    bias=kb_col[:, t : t + 1], scale=ts_col[:, t : t + 1],
                )
            return sig

        def by_run(rows):
            return rows[:].rearrange("p t (c i) -> p c t i", i=RUN)

        def by_word(woven):
            return woven[:].rearrange("p (c i) t -> p c t i", i=RUN)

        def weave_on_vector(sig):
            y_bf = tile([P, HALF, PACK], BF16, "y_bf0", after="v_win1")
            factor = us_col[:].unsqueeze(1).unsqueeze(3).to_broadcast([P, HALF // RUN, PACK, RUN])
            nc.vector.tensor_tensor(by_word(y_bf), by_run(sig), factor, ALU.mult)
            return y_bf

        def weave_on_scalar(sig):
            y_flat = tile([P, PACK, HALF], BF16, "y_flat")
            for t in range(PACK):
                nc.scalar.activation(y_flat[:, t, :], sig[:, t, :], ACT.Copy, scale=us_col[:, t : t + 1])
            y_bf = tile([P, HALF, PACK], BF16, "y_bf1")
            nc.scalar.copy(by_word(y_bf), by_run(y_flat))
            return y_bf

        def pick_values(j):
            picked = tile([P, N], BF16, "v_picked%d" % j, after="q_bf1" if j == 0 else None)
            nc.vector.tensor_copy(picked[:], v_win[j][:].indirect(offsets[:]))
            pairs = picked[:].bitcast(F32)
            turned = ps.tile([P, 2, P], F32, name="v_turned%d" % j, tag=("bank1", "bank2", "v_bank0", "v_bank1")[j])
            for u in range(2):
                nc.tensor.transpose(turned[:, u, :], pairs[:, u : N // 2 : 2], ident[:])
            return turned

        def lay_values(turned, dst):
            nc.scalar.copy(
                dst.bitcast(F32).rearrange("p (e u) -> p e u", u=2), turned[:].rearrange("p u e -> p e u")
            )

        sig0 = sigmoids(0)
        sig1 = sigmoids(1)
        turned0 = pick_values(0)
        turned1 = pick_values(1)
        v_bf01 = tile([P, 2 * N], BF16, "v_bf01")
        lay_values(turned0, v_bf01[:, 0:N])
        lay_values(turned1, v_bf01[:, N : 2 * N])
        y_bf0 = weave_on_vector(sig0)
        y_bf1 = weave_on_scalar(sig1)
        turned2 = pick_values(2)
        codes_a = tile([P, HALF + 2 * P], U32, "codes_a", after="v_win2")
        yq = [quantise(flat(y_bf0), codes_a[:, 0:HALF], "y0")]
        vq01 = quantise(v_bf01[:], codes_a[:, HALF : HALF + 2 * P], "v01")
        turned3 = pick_values(3)
        y_code1 = tile([P, HALF], U32, "y_code1", after="v_win3")
        yq.append(quantise(flat(y_bf1), y_code1[:], "y1"))

        def product(dst, m, vq):
            y_code, y_scale = yq[m // 2]
            cols = slice(P * (m % 2), P * (m % 2 + 1))
            nc.tensor.matmul_mx(
                dst, y_code[:, cols].bitcast(FP8X4), y_scale[:, cols],
                vq[0].bitcast(FP8X4), vq[1][:], start=True, stop=True,
            )

        out_rows = out[0].rearrange("(m p) e -> p m e", p=P)
        low, high = slice(0, 2 * P), slice(2 * P, DV)

        def make_gate(m):
            nc.scalar.activation(gate[:, m, DV - og_raw[m].shape[1] : DV], og_raw[m][:], ACT.Sigmoid)

        def gated(name, acc, rows, cols):
            res = tile(list(acc.shape), F32, name)
            nc.vector.scalar_tensor_tensor(res[:], acc, 1.0 / 16.0, gate[:, rows, cols], ALU.mult, ALU.mult)
            nc.sync.dma_start(out_rows[:, rows, cols], res[:])

        def pair_block(name, bank, vq):
            acc = ps.tile([P, 2, 2 * P], F32, name=name, tag=bank)
            for m in range(2):
                product(acc[:, m, :], m, vq)
            return acc

        make_gate(0)
        make_gate(1)
        acc01_low = pair_block("acc01_low", "bank0", vq01)
        acc2_low = ps.tile([P, 2 * P], F32, name="acc2_low", tag="bank1")
        product(acc2_low[:], 2, vq01)
        acc3 = ps.tile([P, DV], F32, name="acc3", tag="bank3")
        product(acc3[:, low], 3, vq01)
        gated("res01_low", acc01_low[:], slice(0, 2), low)
        v_bf23 = tile([P, 2 * N], BF16, "v_bf23", after="og_raw1")
        lay_values(turned2, v_bf23[:, 0:N])
        lay_values(turned3, v_bf23[:, N : 2 * N])
        v_code23 = tile([P, 2 * P], U32, "v_code23")
        vq23 = quantise(v_bf23[:], v_code23[:], "v23")
        make_gate(2)
        make_gate(3)
        acc01_high = pair_block("acc01_high", "bank2", vq23)
        acc2_high = ps.tile([P, 2 * P], F32, name="acc2_high", tag="ts_bank")
        product(acc2_high[:], 2, vq23)
        product(acc3[:, high], 3, vq23)
        gated("res2_low", acc2_low[:], 2, low)
        gated("res01_high", acc01_high[:], slice(0, 2), high)
        gated("res2_high", acc2_high[:], 2, high)
        gated("res3", acc3[:], 3, slice(0, DV))
